import numpy as np
import ml_dtypes


def mxq(x, axis, fmt="e4m3"):
    dtype, down = {"e4m3": (ml_dtypes.float8_e4m3fn, 7), "e5m2": (ml_dtypes.float8_e5m2, 14)}[fmt]
    v = np.moveaxis(np.asarray(x, np.float32).astype(ml_dtypes.bfloat16).astype(np.float64), axis, -1)
    blocks = v.reshape(v.shape[:-1] + (-1, 32))
    amax = np.abs(blocks).max(-1, keepdims=True)
    byte = np.maximum(np.where(amax > 0, np.frexp(amax)[1] - 1 + 127, 0) - down, 1)
    scale = np.exp2(byte - 127.0)
    codes = (blocks / scale).astype(np.float32).astype(dtype).astype(np.float64)
    return np.moveaxis((codes * scale).reshape(v.shape), -1, axis)


WIDE = False


def mx_kscale(k):
    if not WIDE:
        return np.ones(k)
    levels = np.array([10, -10, 5, -5, 0])
    if k % 512:
        return np.exp2(np.random.permutation(np.resize(levels, k // 32))).repeat(32)
    a = np.empty((k // 512, 16))
    for p in range(k // 512):
        a[p, :8] = np.random.permutation(np.resize(levels, 8))
        for g in range(8):
            far = levels[np.abs(levels - a[p, g]) >= 10]
            a[p, g + 8] = far[np.random.randint(len(far))]
    return np.exp2(a.ravel()).repeat(32)


def f64(x):
    return np.asarray(x).astype(np.float64)


def striped(idx):
    return np.tile(np.asarray(idx).reshape(-1, 16).T, (8, 1)).astype(np.uint16)


def unstriped(offs):
    return offs[:16].T.reshape(-1).astype(np.int64)


E2M1 = np.array([0.0, 0.5, 1.0, 1.5, 2.0, 3.0, 4.0, 6.0, -0.0, -0.5, -1.0, -1.5, -2.0, -3.0, -4.0, -6.0])


def pack_weight(w, fmt):
    k, n = w.shape
    w = f64(np.asarray(w, np.float32).astype(ml_dtypes.bfloat16)).reshape(k // 32, 32, n)
    amax = np.abs(w).max(1)
    if fmt == "e4m3":
        byte = np.frexp(amax)[1] - 1 + 127 - 7
    else:
        mant, ex = np.frexp(amax / 6.0)
        byte = np.where(mant > 0.5, ex, ex - 1) + 127
    byte = np.clip(np.where(amax > 0, byte, 1), 1, 254)
    scaled = (w * np.exp2(127.0 - byte)[:, None, :]).reshape(k, n).astype(np.float32)
    by_word = np.ascontiguousarray(scaled.reshape(k // 512, 128, 4, n).transpose(0, 1, 3, 2))
    if fmt == "e4m3":
        words = by_word.astype(ml_dtypes.float8_e4m3fn).view(np.uint8)
    else:
        c = by_word.astype(ml_dtypes.float4_e2m1fn).view(np.uint8) & 0xF
        words = (c[..., 0::2] | (c[..., 1::2] << 4)).reshape(k // 512, 128, 2 * n)
    return np.ascontiguousarray(words), np.ascontiguousarray(byte.astype(np.uint8).reshape(k // 512, 16, n))


def unpack_weight(words, scales, fmt):
    g, _, n = scales.shape
    words = np.ascontiguousarray(words).reshape(g, 128, n, -1)
    if fmt == "e4m3":
        vals = words.view(ml_dtypes.float8_e4m3fn).astype(np.float64)
    else:
        nib = np.empty((g, 128, n, 4), np.uint8)
        nib[..., 0::2] = words & 0xF
        nib[..., 1::2] = words >> 4
        vals = E2M1[nib]
    vals = vals * np.repeat(np.exp2(scales.astype(np.float64) - 127.0), 8, axis=1)[..., None]
    return vals.transpose(0, 1, 3, 2).reshape(g * 512, n)


D, E, T, I, Q, U = 512, 512, 2048, 256, 512, 1024


def setup_inputs():
    n = np.random.standard_normal
    idx = np.random.permutation(T)[:I]
    idx4 = np.random.permutation(U)[:I]
    fd = mx_kscale(D)
    fe = mx_kscale(E)
    fq = mx_kscale(Q)
    keysp = pack_weight(n((D, T)) / fd[:, None], "e2m1")
    valsp = pack_weight(n((E, T)) / fe[:, None], "e2m1")
    return {
        "query": (n((D, Q)) * 0.6 / np.sqrt(D) * fd[:, None]).astype(np.float32),
        "keys_words": keysp[0],
        "keys_scales": keysp[1],
        "lprior": np.tile(np.random.uniform(-7.5, -5.0, T), (128, 1)).astype(np.float32),
        "strict": (np.random.uniform(0.2, 0.8, (Q, 1))).astype(np.float32),
        "gout": (n((E, Q)) * 1 / np.sqrt(E) * fe[:, None]).astype(np.float32),
        "vals_words": valsp[0],
        "vals_scales": valsp[1],
        "qs": (np.random.uniform(100.0, 400.0, (Q, 1)) * fq[:, None]).astype(np.float32),
        "qrows": (n((Q, D)) / fq[:, None]).astype(np.float32),
        "old": (n((D, U)) * 4.0).astype(np.float32),
        "fade": (np.random.uniform(0.5, 1.0, (1, U))).astype(np.float32),
        "offs": striped(idx),
        "offs4": striped(idx4),
    }


def reference(query, keys_words, keys_scales, lprior, strict, gout, vals_words, vals_scales, qs, qrows, old, fade, offs, offs4):
    idx = unstriped(offs)
    idx4 = unstriped(offs4)
    keysu = unpack_weight(keys_words, keys_scales, "e2m1")
    valsu = unpack_weight(vals_words, vals_scales, "e2m1")
    queryq = mxq(f64(query), 0, "e4m3")
    keysidxg = keysu[:, idx]
    a = queryq.T @ keysidxg
    b = a - np.max(a, axis=1, keepdims=True)
    p = np.exp(b)
    z = np.sum(p, axis=1, keepdims=True)
    goutq = mxq(f64(gout), 0, "e4m3")
    valsidxg = valsu[:, idx]
    c0 = goutq.T @ valsidxg
    dz = f64(strict) / z - np.sum(p * c0, axis=1, keepdims=True) / np.square(z) - f64(strict) * (-1.0) * np.sum(p * (b - f64(lprior)[:1][:, idx]), axis=1, keepdims=True) / np.square(z)
    dp = 1.0 / z * c0 + f64(strict) * (-1.0) / z * (b - f64(lprior)[:1][:, idx]) + dz
    db = f64(strict) * (-1.0) / z * p + dp * p
    gs = db * f64(qs)
    qrowsq = mxq(f64(qrows), 0, "e4m3")
    gsq = mxq(gs, 0, "e4m3")
    gk = qrowsq.T @ gsq
    gf = np.zeros((D, U))
    gf[:, idx4] = gk
    y = f64(old) * f64(fade) + gf
    return y

@@ -1,0 +1,247 @@
+from contextlib import ExitStack
+
+import concourse.mybir as mybir
+from concourse.masks import make_identity
+
+D, E, T, I, Q, U = 512, 512, 2048, 256, 512, 1024
+FLOPS = 2 * (D * Q * I + E * Q * I + Q * D * I)
+BYTES = 4 * (D * Q + E * Q + Q * D + 2 * D * U + T + U + 2 * Q) + 2 * (128 * 2 * T + 16 * T) + 2 * 128 * 16 * 2
+
+F32 = mybir.dt.float32
+BF16 = mybir.dt.bfloat16
+I32 = mybir.dt.int32
+U32 = mybir.dt.uint32
+U16 = mybir.dt.uint16
+U8 = mybir.dt.uint8
+FP8X4 = mybir.dt.float8_e4m3fn_x4
+FP4X4 = mybir.dt.float4_e2m1fn_x4
+ALU = mybir.AluOpType
+ACT = mybir.ActivationFunctionType
+AX = mybir.AxisListType
+
+P = 128
+PACK = 4
+BANK = 512
+
+
+def tile_attend_bpriorpull_k_kernel(tc, query, keys_words, keys_scales, lprior, strict, gout, vals_words,
+                                     vals_scales, qs, qrows, old, fade, offs, offs4, out):
+    nc = tc.nc
+    with ExitStack() as ctx:
+        keep = ctx.enter_context(tc.tile_pool(name="keep", bufs=1))
+        psum = ctx.enter_context(tc.psum_pool(name="psum", bufs=1))
+
+        def sb(name, shape, dtype):
+            return keep.tile(shape, dtype, name=name, align_bytes=64)
+
+        def bank(tag, name):
+            return psum.tile([P, BANK], F32, name=name, tag=tag)
+
+        slot_list = keep.tile([P, I // 16], U16, name="slot_list")
+        place_list = keep.tile([P, I // 16], U16, name="place_list")
+
+        key_bytes = sb("key_bytes", [P, T], U8)
+        val_bytes = sb("val_bytes", [P, T], U8)
+        prior_pool = sb("prior_pool", [P, T], F32)
+        fade_rows = sb("fade_rows", [P, P], F32)
+        placed = [sb("placed%d" % j, [P, U], F32) for j in range(2)]
+        ident = sb("ident", [P, P], F32)
+        warm = sb("warm", [P, 8], F32)
+
+        nc.vector.memset(key_bytes[:].bitcast(I32), 0)
+        nc.vector.memset(val_bytes[:].bitcast(I32), 0)
+        nc.gpsimd.memset(prior_pool[:], 0.0)
+        nc.gpsimd.memset(warm[:], 0.0)
+        nc.gpsimd.memset(fade_rows[:], 0.0)
+        make_identity(nc, ident[:])
+        nc.vector.memset(placed[0][:], 0.0)
+        nc.gpsimd.memset(placed[1][:], 0.0)
+        nc.scalar.activation(out=warm[:, 0:1], in_=warm[:, 1:2], func=ACT.Exp)
+
+        def load_scale_rows(tile, scales):
+            for g in range(4):
+                nc.sync.dma_start(out=tile[32 * g : 32 * g + 4, :].bitcast(I32),
+                                  in_=scales[0, 4 * g : 4 * g + 4, :].bitcast(I32))
+
+        def load_halves(name, src):
+            rows = src.rearrange("(p t) c -> p t c", t=PACK)
+            halves = []
+            for h in range(2):
+                half = sb("%s%d" % (name, h), [P, PACK, 256], F32)
+                nc.sync.dma_start(out=half[:], in_=rows[:, :, 256 * h : 256 * (h + 1)])
+                halves.append(half)
+            return halves
+
+        key_words = sb("key_words", [P, T], U16)
+        val_words = sb("val_words", [P, T], U16)
+        nc.sync.dma_start(out=slot_list[:], in_=offs)
+        query_raw = load_halves("query_raw", query)
+        load_scale_rows(key_bytes, keys_scales)
+        nc.sync.dma_start(out=key_words[:].bitcast(I32), in_=keys_words[0].bitcast(I32))
+        nc.sync.dma_start(out=prior_pool[0:1, :], in_=lprior[0:1, :])
+        load_scale_rows(val_bytes, vals_scales)
+        strict_sb = sb("strict_sb", [P, PACK], F32)
+        qs_sb = sb("qs_sb", [P, PACK], F32)
+        nc.sync.dma_start(out=strict_sb[:], in_=strict.rearrange("(p r) o -> p (r o)", r=PACK))
+        nc.sync.dma_start(out=qs_sb[:], in_=qs.rearrange("(p r) o -> p (r o)", r=PACK))
+        gout_raw = load_halves("gout_raw", gout)
+        nc.sync.dma_start(out=val_words[:].bitcast(I32), in_=vals_words[0].bitcast(I32))
+        nc.sync.dma_start(out=fade_rows[0:8, :], in_=fade.rearrange("o (c p) -> (o c) p", p=P))
+        nc.sync.dma_start(out=place_list[:], in_=offs4)
+        qrows_raw = load_halves("qrows_raw", qrows)
+        old_view = old.rearrange("(j p) u -> p j u", p=P)
+        old_sb = []
+        for h in range(4):
+            part = sb("old%d" % h, [P, PACK, 256], F32)
+            nc.sync.dma_start(out=part[:], in_=old_view[:, :, 256 * h : 256 * (h + 1)])
+            old_sb.append(part)
+
+        def gather(name, pool_tile, dtype):
+            picked = sb(name, [P, I], dtype)
+            nc.vector.tensor_copy(out=picked[:], in_=pool_tile[:].indirect(slot_list[:]))
+            return picked
+
+        def quantise(name, grouped, words):
+            codes = sb(name + "_codes", [P, words], U32)
+            scales = sb(name + "_scales", [P, words], U8)
+            nc.vector.quantize_mx(out=codes[:].bitcast(FP8X4), scales=scales[:], in_=grouped[:])
+            return codes, scales
+
+        def deal(name, halves, copies):
+            grouped = sb(name, [P, PACK * Q], BF16)
+            view = grouped[:].rearrange("p (r s t) -> p s t r", r=PACK, t=PACK)
+            for h in range(2):
+                copies[h](out=view[:, 64 * h : 64 * (h + 1)],
+                          in_=halves[h][:].rearrange("p t (s r) -> p s t r", r=PACK))
+            return grouped
+
+        key_s = gather("key_s", key_bytes, U8)
+        q_codes, q_scales = quantise("q", deal("q_bf", query_raw, (nc.scalar.copy, nc.vector.tensor_copy)), Q)
+        key_w = gather("key_w", key_words, U16)
+
+        def scores(tags, name, codes, scales, words, word_scales):
+            banks = [bank(tags[h], "%s%d" % (name, h)) for h in range(2)]
+            tiles = []
+            for r in range(PACK):
+                dst = banks[r // 2][:, I * (r % 2) : I * (r % 2 + 1)]
+                nc.tensor.matmul_mx(out=dst, lhsT=codes[:, P * r : P * (r + 1)].bitcast(FP8X4),
+                                    lhsT_scale=scales[:, P * r : P * (r + 1)], rhs=words[:].bitcast(FP4X4),
+                                    rhs_scale=word_scales[:], start=True, stop=True)
+                tiles.append(dst)
+            return banks, tiles
+
+        a_banks, a = scores(("A0", "A1"), "a", q_codes, q_scales, key_w, key_s)
+
+        prior_g = gather("prior_g", prior_pool, F32)
+        val_s = gather("val_s", val_bytes, U8)
+
+        turn = bank("T0", "turn")
+        for h in range(2):
+            nc.tensor.transpose(turn[:, P * h : P * (h + 1)], prior_g[:, P * h : P * (h + 1)], ident[:])
+        nc.tensor.transpose(turn[:, 2 * P : 3 * P], fade_rows[:], ident[:])
+        prior_col = sb("prior_col", [P, 2], F32)
+        nc.scalar.copy(out=prior_col[:], in_=turn[:, 0 : 2 * P : P])
+        fade_col = sb("fade_col", [P, 8], F32)
+        nc.scalar.copy(out=fade_col[:], in_=turn[:, 2 * P : 2 * P + 8])
+        spread = bank("T1", "spread")
+        for h in range(2):
+            nc.tensor.transpose(spread[:, P * h : P * (h + 1)], prior_col[:, h : h + 1].to_broadcast([P, P]), ident[:])
+
+        prior_b = sb("prior_b", [P, I], F32)
+        nc.scalar.copy(out=prior_b[:], in_=spread[:, 0:I])
+        neg_strict = sb("neg_strict", [P, PACK], F32)
+        nc.vector.tensor_scalar(out=neg_strict[:], in0=strict_sb[:], scalar1=-1.0, scalar2=None, op0=ALU.mult)
+
+        neg_max = sb("neg_max", [P, PACK], F32)
+        z = sb("z", [P, PACK], F32)
+        p = sb("p", [P, PACK, I], F32)
+        for h in range(2):
+            nc.vector.tensor_reduce(out=neg_max[:, 2 * h : 2 * h + 2],
+                                    in_=a_banks[h][:].rearrange("p (r i) -> p r i", r=2),
+                                    axis=AX.X, op=ALU.max, negate=True)
+        for r in range(PACK):
+            nc.scalar.activation(out=p[:, r, :], in_=a[r], func=ACT.Exp, bias=neg_max[:, r : r + 1],
+                                 accum_out=z[:, r : r + 1])
+
+        g_codes, g_scales = quantise("g", deal("g_bf", gout_raw, (nc.scalar.copy, nc.vector.tensor_copy)), Q)
+        val_w = gather("val_w", val_words, U16)
+        c_banks, c0 = scores(("C0", "C1"), "c", g_codes, g_scales, val_w, val_s)
+
+        u = sb("u", [P, PACK, I], F32)
+        for h in range(2):
+            nc.vector.tensor_tensor(out=u[:, 2 * h : 2 * h + 2, :], in0=a_banks[h][:].rearrange("p (r i) -> p r i", r=2),
+                                    in1=prior_b[:].unsqueeze(1).to_broadcast([P, 2, I]), op=ALU.subtract)
+        inv_z = sb("inv_z", [P, PACK], F32)
+        nc.vector.reciprocal(out=inv_z[:], in_=z[:])
+        row_scale = sb("row_scale", [P, PACK], F32)
+        hq = sb("hq", [P, PACK, I], F32)
+        for r in range(PACK):
+            nc.vector.scalar_tensor_tensor(out=hq[:, r, :], in0=u[:, r, :], scalar=neg_strict[:, r : r + 1],
+                                           in1=c0[r], op0=ALU.mult, op1=ALU.add)
+            if r == 0:
+                nc.vector.tensor_tensor(out=row_scale[:], in0=inv_z[:], in1=qs_sb[:], op=ALU.mult)
+
+        rows_bf = sb("rows_bf", [P, PACK * D], BF16)
+        rows_view = rows_bf[:].rearrange("p (c i t) -> p c t i", i=4, t=PACK)
+        for h in range(2):
+            nc.scalar.copy(out=rows_view[:, 64 * h : 64 * (h + 1)],
+                           in_=qrows_raw[h][:].rearrange("p t (c i) -> p c t i", i=4))
+
+        ph = sb("ph", [P, PACK, I], F32)
+        mean = sb("mean", [P, PACK], F32)
+        for r in range(PACK):
+            nc.vector.scalar_tensor_tensor(out=ph[:, r, :], in0=hq[:, r, :], scalar=row_scale[:, r : r + 1],
+                                           in1=p[:, r, :], op0=ALU.mult, op1=ALU.mult,
+                                           accum_out=mean[:, r : r + 1])
+        r_codes, r_scales = quantise("r", rows_bf, D)
+        back = sb("back", [P, PACK], F32)
+        nc.vector.scalar_tensor_tensor(out=back[:], in0=mean[:], scalar=-1.0, in1=inv_z[:],
+                                       op0=ALU.mult, op1=ALU.mult)
+        gs = sb("gs", [P, PACK, I], BF16)
+        for r in range(PACK):
+            nc.vector.scalar_tensor_tensor(out=gs[:, r, :], in0=p[:, r, :], scalar=back[:, r : r + 1],
+                                           in1=ph[:, r, :], op0=ALU.mult, op1=ALU.add)
+        gs_bf = sb("gs_bf", [P, PACK * I], BF16)
+        nc.vector.tensor_copy(out=gs_bf[:].rearrange("p (c i r) -> p c r i", i=4, r=PACK),
+                              in_=gs[:].rearrange("p r (c i) -> p c r i", i=4))
+        gs_codes, gs_scales = quantise("gs", gs_bf, I)
+
+        faded_t = sb("faded_t", [P, 8, D], F32)
+        stage_tags = ("T2", "T3", "T0", "T1")
+        for c in range(8):
+            stage = bank(stage_tags[c % 4], "stage%d" % c)
+            for j in range(PACK):
+                nc.tensor.transpose(stage[:, P * j : P * (j + 1)],
+                                    old_sb[c // 2][:, j, P * (c % 2) : P * (c % 2 + 1)], ident[:])
+            nc.scalar.activation(out=faded_t[:, c, :], in_=stage[:], func=ACT.Copy, scale=fade_col[:, c : c + 1])
+
+        gk_sb = []
+        for j, tag in enumerate(("A0", "A1", "C0", "C1")):
+            acc = bank(tag, "gk%d" % j)
+            nc.tensor.matmul_mx(out=acc[:, 0:I], lhsT=r_codes[:, P * j : P * (j + 1)].bitcast(FP8X4),
+                                lhsT_scale=r_scales[:, P * j : P * (j + 1)], rhs=gs_codes[:].bitcast(FP8X4),
+                                rhs_scale=gs_scales[:], start=True, stop=True)
+            gk = sb("gk_sb%d" % j, [P, I], F32)
+            nc.scalar.copy(out=gk[:], in_=acc[:, 0:I])
+            gk_sb.append(gk)
+
+        back_tags = (("T0", "T1"), ("T2", "T3"), ("A0", "A1"), ("C0", "C1"))
+
+        def scatter(j):
+            nc.vector.tensor_copy(out=placed[j % 2][:].indirect(place_list[:]), in_=gk_sb[j][:])
+
+        def finish(j):
+            for h in range(2):
+                faded = bank(back_tags[j][h], "faded%d_%d" % (j, h))
+                for c in range(4):
+                    nc.tensor.transpose(faded[:, P * c : P * (c + 1)],
+                                        faded_t[:, 4 * h + c, P * j : P * (j + 1)], ident[:])
+                y = sb("y%d_%d" % (j, h), [P, BANK], F32)
+                nc.vector.tensor_tensor(out=y[:], in0=faded[:], in1=placed[j % 2][:, BANK * h : BANK * (h + 1)], op=ALU.add)
+                nc.sync.dma_start(out=out[P * j : P * (j + 1), BANK * h : BANK * (h + 1)], in_=y[:])
+
+        scatter(0)
+        for j in range(PACK):
+            if j + 1 < PACK:
+                scatter(j + 1)
+            finish(j)

@@ -44,57 +44,56 @@ def tile_attend_bpriorpull_k_kernel(tc, query, keys_words, keys_scales, lprior, 
         val_bytes = sb("val_bytes", [P, T], U8)
         prior_pool = sb("prior_pool", [P, T], F32)
         fade_rows = sb("fade_rows", [P, P], F32)
-        placed = [sb("placed%d" % j, [P, U], F32) for j in range(2)]
+        placed = [sb("placed%d" % j, [P, U], F32) for j in range(PACK)]
         ident = sb("ident", [P, P], F32)
         warm = sb("warm", [P, 8], F32)
 
-        nc.vector.memset(key_bytes[:].bitcast(I32), 0)
-        nc.vector.memset(val_bytes[:].bitcast(I32), 0)
-        nc.gpsimd.memset(prior_pool[:], 0.0)
+        nc.vector.memset(prior_pool[:], 0.0)
         nc.gpsimd.memset(warm[:], 0.0)
         nc.gpsimd.memset(fade_rows[:], 0.0)
         make_identity(nc, ident[:])
-        nc.vector.memset(placed[0][:], 0.0)
-        nc.gpsimd.memset(placed[1][:], 0.0)
+        for window in placed:
+            nc.gpsimd.memset(window[:], 0.0)
         nc.scalar.activation(out=warm[:, 0:1], in_=warm[:, 1:2], func=ACT.Exp)
 
         def load_scale_rows(tile, scales):
             for g in range(4):
-                nc.sync.dma_start(out=tile[32 * g : 32 * g + 4, :].bitcast(I32),
-                                  in_=scales[0, 4 * g : 4 * g + 4, :].bitcast(I32))
+                rows = scales[0, 4 * g : 4 * g + 4, :].bitcast(I32)
+                nc.sync.dma_start(out=tile[32 * g : 32 * (g + 1), :].bitcast(I32),
+                                  in_=rows.unsqueeze(0).to_broadcast([8, 4, T // 4]))
 
-        def load_halves(name, src):
-            rows = src.rearrange("(p t) c -> p t c", t=PACK)
-            halves = []
-            for h in range(2):
-                half = sb("%s%d" % (name, h), [P, PACK, 256], F32)
-                nc.sync.dma_start(out=half[:], in_=rows[:, :, 256 * h : 256 * (h + 1)])
-                halves.append(half)
-            return halves
+        def load_half(name, src, h):
+            half = keep.tile([P, PACK, 256], F32, name="%s%d" % (name, h), tag="%s%d" % (name, h), align_bytes=64)
+            nc.sync.dma_start(out=half[:], in_=src.rearrange("(p t) c -> p t c", t=PACK)[:, :, 256 * h : 256 * (h + 1)])
+            return half
 
         key_words = sb("key_words", [P, T], U16)
         val_words = sb("val_words", [P, T], U16)
-        nc.sync.dma_start(out=slot_list[:], in_=offs)
-        query_raw = load_halves("query_raw", query)
-        load_scale_rows(key_bytes, keys_scales)
-        nc.sync.dma_start(out=key_words[:].bitcast(I32), in_=keys_words[0].bitcast(I32))
-        nc.sync.dma_start(out=prior_pool[0:1, :], in_=lprior[0:1, :])
-        load_scale_rows(val_bytes, vals_scales)
         strict_sb = sb("strict_sb", [P, PACK], F32)
         qs_sb = sb("qs_sb", [P, PACK], F32)
-        nc.sync.dma_start(out=strict_sb[:], in_=strict.rearrange("(p r) o -> p (r o)", r=PACK))
-        nc.sync.dma_start(out=qs_sb[:], in_=qs.rearrange("(p r) o -> p (r o)", r=PACK))
-        gout_raw = load_halves("gout_raw", gout)
+        nc.sync.dma_start(out=slot_list[:], in_=offs)
+        prior_row = sb("prior_row", [1, T], F32)
+        nc.sync.dma_start(out=prior_row[:], in_=lprior[0:1, :])
+        query_raw = [load_half("query_raw", query, 0)]
+        load_scale_rows(key_bytes, keys_scales)
+        query_raw.append(load_half("query_raw", query, 1))
+        nc.sync.dma_start(out=key_words[:].bitcast(I32), in_=keys_words[0].bitcast(I32))
         nc.sync.dma_start(out=val_words[:].bitcast(I32), in_=vals_words[0].bitcast(I32))
+        gout_raw = [load_half("gout_raw", gout, 0)]
+        load_scale_rows(val_bytes, vals_scales)
+        gout_raw.append(load_half("gout_raw", gout, 1))
+        qrows_raw = [load_half("qrows_raw", qrows, 0)]
+        nc.sync.dma_start(out=strict_sb[:], in_=strict.rearrange("(p r) o -> p (r o)", r=PACK))
+        qrows_raw.append(load_half("qrows_raw", qrows, 1))
+        nc.sync.dma_start(out=qs_sb[:], in_=qs.rearrange("(p r) o -> p (r o)", r=PACK))
         nc.sync.dma_start(out=fade_rows[0:8, :], in_=fade.rearrange("o (c p) -> (o c) p", p=P))
-        nc.sync.dma_start(out=place_list[:], in_=offs4)
-        qrows_raw = load_halves("qrows_raw", qrows)
         old_view = old.rearrange("(j p) u -> p j u", p=P)
         old_sb = []
         for h in range(4):
-            part = sb("old%d" % h, [P, PACK, 256], F32)
+            part = keep.tile([P, PACK, 256], F32, name="old%d" % h, tag="old%d" % h, align_bytes=64)
             nc.sync.dma_start(out=part[:], in_=old_view[:, :, 256 * h : 256 * (h + 1)])
             old_sb.append(part)
+        nc.sync.dma_start(out=place_list[:], in_=offs4)
 
         def gather(name, pool_tile, dtype):
             picked = sb(name, [P, I], dtype)
@@ -108,15 +107,18 @@ def tile_attend_bpriorpull_k_kernel(tc, query, keys_words, keys_scales, lprior, 
             return codes, scales
 
         def deal(name, halves, copies):
-            grouped = sb(name, [P, PACK * Q], BF16)
-            view = grouped[:].rearrange("p (r s t) -> p s t r", r=PACK, t=PACK)
+            grouped = keep.tile([P, PACK * Q], BF16, name=name, tag=name, align_bytes=64)
+            view = grouped[:].rearrange("p (r s e t) -> p s t e r", r=PACK, e=2, t=PACK)
             for h in range(2):
-                copies[h](out=view[:, 64 * h : 64 * (h + 1)],
-                          in_=halves[h][:].rearrange("p t (s r) -> p s t r", r=PACK))
+                copies[h](out=view[:, 32 * h : 32 * (h + 1)],
+                          in_=halves[h][:].rearrange("p t (s e r) -> p s t e r", e=2, r=PACK))
             return grouped
 
+        nc.vector.tensor_copy(out=prior_pool[0:1, :], in_=prior_row[:])
+        prior_g = gather("prior_g", prior_pool, F32)
         key_s = gather("key_s", key_bytes, U8)
-        q_codes, q_scales = quantise("q", deal("q_bf", query_raw, (nc.scalar.copy, nc.vector.tensor_copy)), Q)
+        q_bf = deal("q_bf", query_raw, (nc.scalar.copy, nc.vector.tensor_copy))
+        q_codes, q_scales = quantise("q", q_bf, Q)
         key_w = gather("key_w", key_words, U16)
 
         def scores(tags, name, codes, scales, words, word_scales):
@@ -132,42 +134,37 @@ def tile_attend_bpriorpull_k_kernel(tc, query, keys_words, keys_scales, lprior, 
 
         a_banks, a = scores(("A0", "A1"), "a", q_codes, q_scales, key_w, key_s)
 
-        prior_g = gather("prior_g", prior_pool, F32)
-        val_s = gather("val_s", val_bytes, U8)
 
+        val_w = gather("val_w", val_words, U16)
         turn = bank("T0", "turn")
         for h in range(2):
             nc.tensor.transpose(turn[:, P * h : P * (h + 1)], prior_g[:, P * h : P * (h + 1)], ident[:])
-        nc.tensor.transpose(turn[:, 2 * P : 3 * P], fade_rows[:], ident[:])
         prior_col = sb("prior_col", [P, 2], F32)
         nc.scalar.copy(out=prior_col[:], in_=turn[:, 0 : 2 * P : P])
-        fade_col = sb("fade_col", [P, 8], F32)
-        nc.scalar.copy(out=fade_col[:], in_=turn[:, 2 * P : 2 * P + 8])
         spread = bank("T1", "spread")
         for h in range(2):
             nc.tensor.transpose(spread[:, P * h : P * (h + 1)], prior_col[:, h : h + 1].to_broadcast([P, P]), ident[:])
 
         prior_b = sb("prior_b", [P, I], F32)
         nc.scalar.copy(out=prior_b[:], in_=spread[:, 0:I])
-        neg_strict = sb("neg_strict", [P, PACK], F32)
-        nc.vector.tensor_scalar(out=neg_strict[:], in0=strict_sb[:], scalar1=-1.0, scalar2=None, op0=ALU.mult)
 
         neg_max = sb("neg_max", [P, PACK], F32)
         z = sb("z", [P, PACK], F32)
-        p = sb("p", [P, PACK, I], F32)
         for h in range(2):
             nc.vector.tensor_reduce(out=neg_max[:, 2 * h : 2 * h + 2],
                                     in_=a_banks[h][:].rearrange("p (r i) -> p r i", r=2),
                                     axis=AX.X, op=ALU.max, negate=True)
+        val_s = gather("val_s", val_bytes, U8)
+        g_bf = deal("g_bf", gout_raw, (nc.scalar.copy, nc.vector.tensor_copy))
+        p = keep.tile([P, PACK, I], F32, name="p", tag="gout_raw0", align_bytes=64)
         for r in range(PACK):
             nc.scalar.activation(out=p[:, r, :], in_=a[r], func=ACT.Exp, bias=neg_max[:, r : r + 1],
                                  accum_out=z[:, r : r + 1])
 
-        g_codes, g_scales = quantise("g", deal("g_bf", gout_raw, (nc.scalar.copy, nc.vector.tensor_copy)), Q)
-        val_w = gather("val_w", val_words, U16)
+        g_codes, g_scales = quantise("g", g_bf, Q)
         c_banks, c0 = scores(("C0", "C1"), "c", g_codes, g_scales, val_w, val_s)
 
-        u = sb("u", [P, PACK, I], F32)
+        u = keep.tile([P, PACK, I], F32, name="u", tag="g_bf", align_bytes=64)
         for h in range(2):
             nc.vector.tensor_tensor(out=u[:, 2 * h : 2 * h + 2, :], in0=a_banks[h][:].rearrange("p (r i) -> p r i", r=2),
                                     in1=prior_b[:].unsqueeze(1).to_broadcast([P, 2, I]), op=ALU.subtract)
@@ -176,10 +173,11 @@ def tile_attend_bpriorpull_k_kernel(tc, query, keys_words, keys_scales, lprior, 
         row_scale = sb("row_scale", [P, PACK], F32)
         hq = sb("hq", [P, PACK, I], F32)
         for r in range(PACK):
-            nc.vector.scalar_tensor_tensor(out=hq[:, r, :], in0=u[:, r, :], scalar=neg_strict[:, r : r + 1],
-                                           in1=c0[r], op0=ALU.mult, op1=ALU.add)
+            nc.vector.scalar_tensor_tensor(out=hq[:, r, :], in0=u[:, r, :], scalar=strict_sb[:, r : r + 1],
+                                           in1=c0[r], op0=ALU.mult, op1=ALU.subtract)
             if r == 0:
-                nc.vector.tensor_tensor(out=row_scale[:], in0=inv_z[:], in1=qs_sb[:], op=ALU.mult)
+                nc.vector.scalar_tensor_tensor(out=row_scale[:], in0=inv_z[:], scalar=-1.0, in1=qs_sb[:],
+                                               op0=ALU.mult, op1=ALU.mult)
 
         rows_bf = sb("rows_bf", [P, PACK * D], BF16)
         rows_view = rows_bf[:].rearrange("p (c i t) -> p c t i", i=4, t=PACK)
@@ -187,34 +185,55 @@ def tile_attend_bpriorpull_k_kernel(tc, query, keys_words, keys_scales, lprior, 
             nc.scalar.copy(out=rows_view[:, 64 * h : 64 * (h + 1)],
                            in_=qrows_raw[h][:].rearrange("p t (c i) -> p c t i", i=4))
 
-        ph = sb("ph", [P, PACK, I], F32)
-        mean = sb("mean", [P, PACK], F32)
-        for r in range(PACK):
-            nc.vector.scalar_tensor_tensor(out=ph[:, r, :], in0=hq[:, r, :], scalar=row_scale[:, r : r + 1],
-                                           in1=p[:, r, :], op0=ALU.mult, op1=ALU.mult,
-                                           accum_out=mean[:, r : r + 1])
-        r_codes, r_scales = quantise("r", rows_bf, D)
-        back = sb("back", [P, PACK], F32)
-        nc.vector.scalar_tensor_tensor(out=back[:], in0=mean[:], scalar=-1.0, in1=inv_z[:],
-                                       op0=ALU.mult, op1=ALU.mult)
-        gs = sb("gs", [P, PACK, I], BF16)
-        for r in range(PACK):
-            nc.vector.scalar_tensor_tensor(out=gs[:, r, :], in0=p[:, r, :], scalar=back[:, r : r + 1],
-                                           in1=ph[:, r, :], op0=ALU.mult, op1=ALU.add)
-        gs_bf = sb("gs_bf", [P, PACK * I], BF16)
-        nc.vector.tensor_copy(out=gs_bf[:].rearrange("p (c i r) -> p c r i", i=4, r=PACK),
-                              in_=gs[:].rearrange("p r (c i) -> p c r i", i=4))
-        gs_codes, gs_scales = quantise("gs", gs_bf, I)
+        fade_turn = bank("T0", "fade_turn")
+        nc.tensor.transpose(fade_turn[:, 0:P], fade_rows[:], ident[:])
+        fade_col = sb("fade_col", [P, 8], F32)
+        nc.scalar.copy(out=fade_col[:], in_=fade_turn[:, 0:8])
+        faded_t = []
+        stage_tags = ("T2", "T3", "T1", "T0", "A0", "A1", "C0", "C1")
+        faded_tags = ("faded_t0", "gout_raw0", "faded_t2", "faded_t3")
 
-        faded_t = sb("faded_t", [P, 8, D], F32)
-        stage_tags = ("T2", "T3", "T0", "T1")
-        for c in range(8):
-            stage = bank(stage_tags[c % 4], "stage%d" % c)
+        def fade_block(c):
+            if c % 2 == 0:
+                faded_t.append(keep.tile([P, 2, D], F32, name="faded_t%d" % (c // 2), tag=faded_tags[c // 2], align_bytes=64))
+            stage = bank(stage_tags[c], "stage%d" % c)
             for j in range(PACK):
                 nc.tensor.transpose(stage[:, P * j : P * (j + 1)],
                                     old_sb[c // 2][:, j, P * (c % 2) : P * (c % 2 + 1)], ident[:])
-            nc.scalar.activation(out=faded_t[:, c, :], in_=stage[:], func=ACT.Copy, scale=fade_col[:, c : c + 1])
+            nc.scalar.activation(out=faded_t[c // 2][:, c % 2, :], in_=stage[:], func=ACT.Copy, scale=fade_col[:, c : c + 1])
 
+        for c in range(2):
+            fade_block(c)
+        pw = keep.tile([P, PACK, I], F32, name="pw", tag="old0", align_bytes=64)
+        ph = sb("ph", [P, PACK, I], F32)
+        mean = sb("mean", [P, PACK], F32)
+        back = sb("back", [P, PACK], F32)
+        for h in range(2):
+            for r in (2 * h, 2 * h + 1):
+                nc.vector.scalar_tensor_tensor(out=ph[:, r, :], in0=hq[:, r, :], scalar=row_scale[:, r : r + 1],
+                                               in1=p[:, r, :], op0=ALU.mult, op1=ALU.mult,
+                                               accum_out=mean[:, r : r + 1])
+            nc.vector.tensor_tensor(out=back[:, 2 * h : 2 * h + 2], in0=mean[:, 2 * h : 2 * h + 2],
+                                    in1=inv_z[:, 2 * h : 2 * h + 2], op=ALU.mult)
+            for r in (2 * h, 2 * h + 1):
+                nc.scalar.activation(out=pw[:, r, :], in_=p[:, r, :], func=ACT.Copy, scale=back[:, r : r + 1])
+        r_codes = sb("r_codes", [P, D], U32)
+        r_scales = sb("r_scales", [P, D], U8)
+
+        def quantise_rows(lo, hi):
+            nc.vector.quantize_mx(out=r_codes[:, lo:hi].bitcast(FP8X4), scales=r_scales[:, lo:hi],
+                                  in_=rows_bf[:, PACK * lo : PACK * hi])
+
+        quantise_rows(0, 256)
+        gs_bf = sb("gs_bf", [P, PACK * I], BF16)
+        nc.vector.tensor_tensor(out=gs_bf[:].rearrange("p (c i r) -> p c r i", i=4, r=PACK),
+                                in0=ph[:].rearrange("p r (c i) -> p c r i", i=4),
+                                in1=pw[:].rearrange("p r (c i) -> p c r i", i=4), op=ALU.subtract)
+        gs_codes, gs_scales = quantise("gs", gs_bf, I)
+        quantise_rows(256, 512)
+
+        for c in range(2, 4):
+            fade_block(c)
         gk_sb = []
         for j, tag in enumerate(("A0", "A1", "C0", "C1")):
             acc = bank(tag, "gk%d" % j)
@@ -225,23 +244,24 @@ def tile_attend_bpriorpull_k_kernel(tc, query, keys_words, keys_scales, lprior, 
             nc.scalar.copy(out=gk[:], in_=acc[:, 0:I])
             gk_sb.append(gk)
 
-        back_tags = (("T0", "T1"), ("T2", "T3"), ("A0", "A1"), ("C0", "C1"))
+        for c in range(4, 8):
+            fade_block(c)
+        back_tags = (("T2", "T3"), ("T1", "T0"), ("A0", "A1"), ("C0", "C1"))
 
         def scatter(j):
-            nc.vector.tensor_copy(out=placed[j % 2][:].indirect(place_list[:]), in_=gk_sb[j][:])
+            nc.vector.tensor_copy(out=placed[j][:].indirect(place_list[:]), in_=gk_sb[j][:])
 
         def finish(j):
             for h in range(2):
                 faded = bank(back_tags[j][h], "faded%d_%d" % (j, h))
                 for c in range(4):
                     nc.tensor.transpose(faded[:, P * c : P * (c + 1)],
-                                        faded_t[:, 4 * h + c, P * j : P * (j + 1)], ident[:])
+                                        faded_t[2 * h + c // 2][:, c % 2, P * j : P * (j + 1)], ident[:])
                 y = sb("y%d_%d" % (j, h), [P, BANK], F32)
-                nc.vector.tensor_tensor(out=y[:], in0=faded[:], in1=placed[j % 2][:, BANK * h : BANK * (h + 1)], op=ALU.add)
+                nc.vector.tensor_tensor(out=y[:], in0=faded[:], in1=placed[j][:, BANK * h : BANK * (h + 1)], op=ALU.add)
                 nc.sync.dma_start(out=out[P * j : P * (j + 1), BANK * h : BANK * (h + 1)], in_=y[:])
 
-        scatter(0)
         for j in range(PACK):
-            if j + 1 < PACK:
-                scatter(j + 1)
+            scatter(j)
+        for j in range(PACK):
             finish(j)

@@ -22,6 +22,9 @@ AX = mybir.AxisListType
 P = 128
 PACK = 4
 BANK = 512
+HALF = 256
+LINE = 4
+WINDOWS = 3
 
 
 def tile_attend_bpriorpull_k_kernel(tc, query, keys_words, keys_scales, lprior, strict, gout, vals_words,
@@ -31,8 +34,8 @@ def tile_attend_bpriorpull_k_kernel(tc, query, keys_words, keys_scales, lprior, 
         keep = ctx.enter_context(tc.tile_pool(name="keep", bufs=1))
         psum = ctx.enter_context(tc.psum_pool(name="psum", bufs=1))
 
-        def sb(name, shape, dtype):
-            return keep.tile(shape, dtype, name=name, align_bytes=64)
+        def sb(name, shape, dtype, reuse=None):
+            return keep.tile(shape, dtype, name=name, tag=reuse or name, align_bytes=64)
 
         def bank(tag, name):
             return psum.tile([P, BANK], F32, name=name, tag=tag)
@@ -44,17 +47,14 @@ def tile_attend_bpriorpull_k_kernel(tc, query, keys_words, keys_scales, lprior, 
         val_bytes = sb("val_bytes", [P, T], U8)
         prior_pool = sb("prior_pool", [P, T], F32)
         fade_rows = sb("fade_rows", [P, P], F32)
-        placed = [sb("placed%d" % j, [P, U], F32) for j in range(PACK)]
+        windows = [sb("window%d" % w, [P, U], F32) for w in range(WINDOWS)]
         ident = sb("ident", [P, P], F32)
-        warm = sb("warm", [P, 8], F32)
 
-        nc.vector.memset(prior_pool[:], 0.0)
-        nc.gpsimd.memset(warm[:], 0.0)
+        nc.vector.memset(prior_pool[:].bitcast(I32), 0)
         nc.gpsimd.memset(fade_rows[:], 0.0)
         make_identity(nc, ident[:])
-        for window in placed:
-            nc.gpsimd.memset(window[:], 0.0)
-        nc.scalar.activation(out=warm[:, 0:1], in_=warm[:, 1:2], func=ACT.Exp)
+        for window in windows:
+            nc.vector.memset(window[:].bitcast(I32), 0)
 
         def load_scale_rows(tile, scales):
             for g in range(4):
@@ -63,8 +63,8 @@ def tile_attend_bpriorpull_k_kernel(tc, query, keys_words, keys_scales, lprior, 
                                   in_=rows.unsqueeze(0).to_broadcast([8, 4, T // 4]))
 
         def load_half(name, src, h):
-            half = keep.tile([P, PACK, 256], F32, name="%s%d" % (name, h), tag="%s%d" % (name, h), align_bytes=64)
-            nc.sync.dma_start(out=half[:], in_=src.rearrange("(p t) c -> p t c", t=PACK)[:, :, 256 * h : 256 * (h + 1)])
+            half = sb("%s%d" % (name, h), [P, PACK, HALF], F32)
+            nc.sync.dma_start(out=half[:], in_=src.rearrange("(p t) c -> p t c", t=PACK)[:, :, HALF * h : HALF * (h + 1)])
             return half
 
         key_words = sb("key_words", [P, T], U16)
@@ -86,12 +86,12 @@ def tile_attend_bpriorpull_k_kernel(tc, query, keys_words, keys_scales, lprior, 
         nc.sync.dma_start(out=strict_sb[:], in_=strict.rearrange("(p r) o -> p (r o)", r=PACK))
         qrows_raw.append(load_half("qrows_raw", qrows, 1))
         nc.sync.dma_start(out=qs_sb[:], in_=qs.rearrange("(p r) o -> p (r o)", r=PACK))
-        nc.sync.dma_start(out=fade_rows[0:8, :], in_=fade.rearrange("o (c p) -> (o c) p", p=P))
+        nc.sync.dma_start(out=fade_rows[0 : U // P, :], in_=fade.rearrange("o (c p) -> (o c) p", p=P))
         old_view = old.rearrange("(j p) u -> p j u", p=P)
         old_sb = []
-        for h in range(4):
-            part = keep.tile([P, PACK, 256], F32, name="old%d" % h, tag="old%d" % h, align_bytes=64)
-            nc.sync.dma_start(out=part[:], in_=old_view[:, :, 256 * h : 256 * (h + 1)])
+        for h in range(2):
+            part = sb("old%d" % h, [P, PACK, BANK], F32)
+            nc.sync.dma_start(out=part[:], in_=old_view[:, :, BANK * h : BANK * (h + 1)])
             old_sb.append(part)
         nc.sync.dma_start(out=place_list[:], in_=offs4)
 
@@ -100,26 +100,19 @@ def tile_attend_bpriorpull_k_kernel(tc, query, keys_words, keys_scales, lprior, 
             nc.vector.tensor_copy(out=picked[:], in_=pool_tile[:].indirect(slot_list[:]))
             return picked
 
-        def quantise(name, grouped, words):
-            codes = sb(name + "_codes", [P, words], U32)
-            scales = sb(name + "_scales", [P, words], U8)
+        def quantise(name, grouped):
+            codes = sb(name + "_codes", [P, Q], U32)
+            scales = sb(name + "_scales", [P, Q], U8)
             nc.vector.quantize_mx(out=codes[:].bitcast(FP8X4), scales=scales[:], in_=grouped[:])
             return codes, scales
 
-        def deal(name, halves, copies):
-            grouped = keep.tile([P, PACK * Q], BF16, name=name, tag=name, align_bytes=64)
-            view = grouped[:].rearrange("p (r s e t) -> p s t e r", r=PACK, e=2, t=PACK)
-            for h in range(2):
-                copies[h](out=view[:, 32 * h : 32 * (h + 1)],
-                          in_=halves[h][:].rearrange("p t (s e r) -> p s t e r", e=2, r=PACK))
+        def deal(name, halves):
+            grouped = sb(name, [P, PACK * Q], BF16)
+            view = grouped[:].rearrange("p (r m e t) -> p m t e r", r=PACK, e=2, t=PACK)
+            for h, copy in enumerate((nc.scalar.copy, nc.vector.tensor_copy)):
+                copy(out=view[:, 32 * h : 32 * (h + 1)],
+                     in_=halves[h][:].rearrange("p t (m e r) -> p m t e r", e=2, r=PACK))
             return grouped
-
-        nc.vector.tensor_copy(out=prior_pool[0:1, :], in_=prior_row[:])
-        prior_g = gather("prior_g", prior_pool, F32)
-        key_s = gather("key_s", key_bytes, U8)
-        q_bf = deal("q_bf", query_raw, (nc.scalar.copy, nc.vector.tensor_copy))
-        q_codes, q_scales = quantise("q", q_bf, Q)
-        key_w = gather("key_w", key_words, U16)
 
         def scores(tags, name, codes, scales, words, word_scales):
             banks = [bank(tags[h], "%s%d" % (name, h)) for h in range(2)]
@@ -132,10 +125,14 @@ def tile_attend_bpriorpull_k_kernel(tc, query, keys_words, keys_scales, lprior, 
                 tiles.append(dst)
             return banks, tiles
 
+        nc.scalar.activation(out=prior_pool[0:1, :], in_=prior_row[:], func=ACT.Copy)
+        key_s = gather("key_s", key_bytes, U8)
+        prior_g = gather("prior_g", prior_pool, F32)
+        q_codes, q_scales = quantise("q", deal("q_bf", query_raw))
+        key_w = gather("key_w", key_words, U16)
         a_banks, a = scores(("A0", "A1"), "a", q_codes, q_scales, key_w, key_s)
-
-
         val_w = gather("val_w", val_words, U16)
+
         turn = bank("T0", "turn")
         for h in range(2):
             nc.tensor.transpose(turn[:, P * h : P * (h + 1)], prior_g[:, P * h : P * (h + 1)], ident[:])
@@ -144,9 +141,8 @@ def tile_attend_bpriorpull_k_kernel(tc, query, keys_words, keys_scales, lprior, 
         spread = bank("T1", "spread")
         for h in range(2):
             nc.tensor.transpose(spread[:, P * h : P * (h + 1)], prior_col[:, h : h + 1].to_broadcast([P, P]), ident[:])
-
-        prior_b = sb("prior_b", [P, I], F32)
-        nc.scalar.copy(out=prior_b[:], in_=spread[:, 0:I])
+        prior_all = sb("prior_all", [P, I], F32)
+        nc.scalar.copy(out=prior_all[:], in_=spread[:, 0:I])
 
         neg_max = sb("neg_max", [P, PACK], F32)
         z = sb("z", [P, PACK], F32)
@@ -155,113 +151,155 @@ def tile_attend_bpriorpull_k_kernel(tc, query, keys_words, keys_scales, lprior, 
                                     in_=a_banks[h][:].rearrange("p (r i) -> p r i", r=2),
                                     axis=AX.X, op=ALU.max, negate=True)
         val_s = gather("val_s", val_bytes, U8)
-        g_bf = deal("g_bf", gout_raw, (nc.scalar.copy, nc.vector.tensor_copy))
-        p = keep.tile([P, PACK, I], F32, name="p", tag="gout_raw0", align_bytes=64)
+        g_bf = deal("g_bf", gout_raw)
+        p = sb("p", [P, PACK, I], F32, reuse="gout_raw0")
         for r in range(PACK):
             nc.scalar.activation(out=p[:, r, :], in_=a[r], func=ACT.Exp, bias=neg_max[:, r : r + 1],
                                  accum_out=z[:, r : r + 1])
+        g_codes, g_scales = quantise("g", g_bf)
+        c0 = scores(("C0", "C1"), "c", g_codes, g_scales, val_w, val_s)[1]
 
-        g_codes, g_scales = quantise("g", g_bf, Q)
-        c_banks, c0 = scores(("C0", "C1"), "c", g_codes, g_scales, val_w, val_s)
-
-        u = keep.tile([P, PACK, I], F32, name="u", tag="g_bf", align_bytes=64)
+        gap = sb("gap", [P, PACK, I], F32, reuse="g_bf")
         for h in range(2):
-            nc.vector.tensor_tensor(out=u[:, 2 * h : 2 * h + 2, :], in0=a_banks[h][:].rearrange("p (r i) -> p r i", r=2),
-                                    in1=prior_b[:].unsqueeze(1).to_broadcast([P, 2, I]), op=ALU.subtract)
+            nc.vector.tensor_tensor(out=gap[:, 2 * h : 2 * h + 2, :], in0=a_banks[h][:].rearrange("p (r i) -> p r i", r=2),
+                                    in1=prior_all[:].unsqueeze(1).to_broadcast([P, 2, I]), op=ALU.subtract)
         inv_z = sb("inv_z", [P, PACK], F32)
         nc.vector.reciprocal(out=inv_z[:], in_=z[:])
-        row_scale = sb("row_scale", [P, PACK], F32)
-        hq = sb("hq", [P, PACK, I], F32)
-        for r in range(PACK):
-            nc.vector.scalar_tensor_tensor(out=hq[:, r, :], in0=u[:, r, :], scalar=strict_sb[:, r : r + 1],
+        neg_scale = sb("neg_scale", [P, PACK], F32)
+        neg_h = sb("neg_h", [P, PACK, I], F32)
+
+        def pull(r):
+            nc.vector.scalar_tensor_tensor(out=neg_h[:, r, :], in0=gap[:, r, :], scalar=strict_sb[:, r : r + 1],
                                            in1=c0[r], op0=ALU.mult, op1=ALU.subtract)
-            if r == 0:
-                nc.vector.scalar_tensor_tensor(out=row_scale[:], in0=inv_z[:], scalar=-1.0, in1=qs_sb[:],
-                                               op0=ALU.mult, op1=ALU.mult)
+
+        pull(0)
+        nc.vector.scalar_tensor_tensor(out=neg_scale[:], in0=inv_z[:], scalar=-1.0, in1=qs_sb[:],
+                                       op0=ALU.mult, op1=ALU.mult)
+        for r in range(1, PACK):
+            pull(r)
 
         rows_bf = sb("rows_bf", [P, PACK * D], BF16)
-        rows_view = rows_bf[:].rearrange("p (c i t) -> p c t i", i=4, t=PACK)
+        rows_view = rows_bf[:].rearrange("p (c i t) -> p c t i", i=LINE, t=PACK)
         for h in range(2):
             nc.scalar.copy(out=rows_view[:, 64 * h : 64 * (h + 1)],
-                           in_=qrows_raw[h][:].rearrange("p t (c i) -> p c t i", i=4))
+                           in_=qrows_raw[h][:].rearrange("p t (c i) -> p c t i", i=LINE))
 
         fade_turn = bank("T0", "fade_turn")
         nc.tensor.transpose(fade_turn[:, 0:P], fade_rows[:], ident[:])
-        fade_col = sb("fade_col", [P, 8], F32)
-        nc.scalar.copy(out=fade_col[:], in_=fade_turn[:, 0:8])
+        fade_col = sb("fade_col", [P, U // P], F32)
+        nc.scalar.copy(out=fade_col[:], in_=fade_turn[:, 0 : U // P])
         faded_t = []
-        stage_tags = ("T2", "T3", "T1", "T0", "A0", "A1", "C0", "C1")
-        faded_tags = ("faded_t0", "gout_raw0", "faded_t2", "faded_t3")
+        stage_tags = ("T2", "T3", "T1", "T0", "T2", "T3", "C0", "C1")
+        faded_reuse = (None, "neg_h", "gout_raw0", None)
 
         def fade_block(c):
             if c % 2 == 0:
-                faded_t.append(keep.tile([P, 2, D], F32, name="faded_t%d" % (c // 2), tag=faded_tags[c // 2], align_bytes=64))
+                faded_t.append(sb("faded_t%d" % (c // 2), [P, 2, D], F32, reuse=faded_reuse[c // 2]))
             stage = bank(stage_tags[c], "stage%d" % c)
             for j in range(PACK):
                 nc.tensor.transpose(stage[:, P * j : P * (j + 1)],
-                                    old_sb[c // 2][:, j, P * (c % 2) : P * (c % 2 + 1)], ident[:])
-            nc.scalar.activation(out=faded_t[c // 2][:, c % 2, :], in_=stage[:], func=ACT.Copy, scale=fade_col[:, c : c + 1])
+                                    old_sb[c // 4][:, j, P * (c % 4) : P * (c % 4 + 1)], ident[:])
+            nc.scalar.activation(out=faded_t[c // 2][:, c % 2, :], in_=stage[:], func=ACT.Copy,
+                                 scale=fade_col[:, c : c + 1])
 
         for c in range(2):
             fade_block(c)
-        pw = keep.tile([P, PACK, I], F32, name="pw", tag="old0", align_bytes=64)
+
+        pm = sb("pm", [P, PACK, I], F32, reuse="qrows_raw1")
         ph = sb("ph", [P, PACK, I], F32)
+        total = sb("total", [P, PACK], F32)
         mean = sb("mean", [P, PACK], F32)
-        back = sb("back", [P, PACK], F32)
-        for h in range(2):
-            for r in (2 * h, 2 * h + 1):
-                nc.vector.scalar_tensor_tensor(out=ph[:, r, :], in0=hq[:, r, :], scalar=row_scale[:, r : r + 1],
-                                               in1=p[:, r, :], op0=ALU.mult, op1=ALU.mult,
-                                               accum_out=mean[:, r : r + 1])
-            nc.vector.tensor_tensor(out=back[:, 2 * h : 2 * h + 2], in0=mean[:, 2 * h : 2 * h + 2],
-                                    in1=inv_z[:, 2 * h : 2 * h + 2], op=ALU.mult)
-            for r in (2 * h, 2 * h + 1):
-                nc.scalar.activation(out=pw[:, r, :], in_=p[:, r, :], func=ACT.Copy, scale=back[:, r : r + 1])
+
+        def weigh(r):
+            nc.vector.scalar_tensor_tensor(out=ph[:, r, :], in0=neg_h[:, r, :], scalar=neg_scale[:, r : r + 1],
+                                           in1=p[:, r, :], op0=ALU.mult, op1=ALU.mult,
+                                           accum_out=total[:, r : r + 1])
+
+        for lo, hi in ((0, 2), (2, 3)):
+            for r in range(lo, hi):
+                weigh(r)
+            nc.vector.tensor_tensor(out=mean[:, lo:hi], in0=total[:, lo:hi], in1=inv_z[:, lo:hi], op=ALU.mult)
+            for r in range(lo, hi):
+                nc.scalar.activation(out=pm[:, r, :], in_=p[:, r, :], func=ACT.Copy, scale=mean[:, r : r + 1])
+        weigh(3)
         r_codes = sb("r_codes", [P, D], U32)
         r_scales = sb("r_scales", [P, D], U8)
 
-        def quantise_rows(lo, hi):
-            nc.vector.quantize_mx(out=r_codes[:, lo:hi].bitcast(FP8X4), scales=r_scales[:, lo:hi],
-                                  in_=rows_bf[:, PACK * lo : PACK * hi])
+        def quantise_rows(h):
+            cols = slice(HALF * h, HALF * (h + 1))
+            nc.vector.quantize_mx(out=r_codes[:, cols].bitcast(FP8X4), scales=r_scales[:, cols],
+                                  in_=rows_bf[:, PACK * cols.start : PACK * cols.stop])
 
-        quantise_rows(0, 256)
+        quantise_rows(0)
+        nc.vector.tensor_scalar(out=pm[:, 3, :], in0=p[:, 3, :], scalar1=total[:, 3:4], scalar2=inv_z[:, 3:4],
+                                op0=ALU.mult, op1=ALU.mult)
+
         gs_bf = sb("gs_bf", [P, PACK * I], BF16)
-        nc.vector.tensor_tensor(out=gs_bf[:].rearrange("p (c i r) -> p c r i", i=4, r=PACK),
-                                in0=ph[:].rearrange("p r (c i) -> p c r i", i=4),
-                                in1=pw[:].rearrange("p r (c i) -> p c r i", i=4), op=ALU.subtract)
-        gs_codes, gs_scales = quantise("gs", gs_bf, I)
-        quantise_rows(256, 512)
+        gs_codes = sb("gs_codes", [P, I], U32)
+        gs_scales = sb("gs_scales", [P, I], U8)
+        for h in range(2):
+            lines = slice(32 * h, 32 * (h + 1))
+            nc.vector.tensor_tensor(out=gs_bf[:].rearrange("p (c i r) -> p c r i", i=LINE, r=PACK)[:, lines],
+                                    in0=ph[:].rearrange("p r (c i) -> p c r i", i=LINE)[:, lines],
+                                    in1=pm[:].rearrange("p r (c i) -> p c r i", i=LINE)[:, lines],
+                                    op=ALU.subtract)
+        for h in range(2):
+            nc.vector.quantize_mx(out=gs_codes[:, P * h : P * (h + 1)].bitcast(FP8X4),
+                                  scales=gs_scales[:, P * h : P * (h + 1)],
+                                  in_=gs_bf[:, PACK * P * h : PACK * P * (h + 1)])
+        quantise_rows(1)
 
-        for c in range(2, 4):
+        for c in range(2, 6):
             fade_block(c)
+
+        pieces = ((0, 0, P), (1, 0, P), (0, P, I), (1, P, I), (2, 0, I), (3, 0, I))
+        piece_tags = ("A0", "A1", "C0", "C1", "A0", "A1")
         gk_sb = []
-        for j, tag in enumerate(("A0", "A1", "C0", "C1")):
-            acc = bank(tag, "gk%d" % j)
-            nc.tensor.matmul_mx(out=acc[:, 0:I], lhsT=r_codes[:, P * j : P * (j + 1)].bitcast(FP8X4),
-                                lhsT_scale=r_scales[:, P * j : P * (j + 1)], rhs=gs_codes[:].bitcast(FP8X4),
-                                rhs_scale=gs_scales[:], start=True, stop=True)
-            gk = sb("gk_sb%d" % j, [P, I], F32)
-            nc.scalar.copy(out=gk[:], in_=acc[:, 0:I])
+        for n, (j, lo, hi) in enumerate(pieces):
+            acc = bank(piece_tags[n], "gk%d" % n)
+            nc.tensor.matmul_mx(out=acc[:, 0 : hi - lo], lhsT=r_codes[:, P * j : P * (j + 1)].bitcast(FP8X4),
+                                lhsT_scale=r_scales[:, P * j : P * (j + 1)], rhs=gs_codes[:, lo:hi].bitcast(FP8X4),
+                                rhs_scale=gs_scales[:, lo:hi], start=True, stop=True)
+            gk = sb("gk_sb%d" % n, [P, hi - lo], F32)
+            nc.scalar.copy(out=gk[:], in_=acc[:, 0 : hi - lo])
             gk_sb.append(gk)
 
-        for c in range(4, 8):
+        def scatter(n):
+            j, lo, hi = pieces[n]
+            nc.vector.tensor_copy(out=windows[j % WINDOWS][:].indirect(place_list[:, lo // 16 : hi // 16]),
+                                  in_=gk_sb[n][:])
+
+        def turn_back(j, h, tag):
+            faded = bank(tag, "faded%d_%d" % (j, h))
+            for c in range(4):
+                nc.tensor.transpose(faded[:, P * c : P * (c + 1)],
+                                    faded_t[2 * h + c // 2][:, c % 2, P * j : P * (j + 1)], ident[:])
+            return faded
+
+        def finish_left(j):
+            faded = turn_back(j, 0, ("A0", "A1", "C0", "C1")[j])
+            y = sb("y_left%d" % j, [P, BANK], F32)
+            faded_sb = sb("faded_sb%d" % j, [P, BANK], F32)
+            nc.scalar.copy(out=faded_sb[:], in_=faded[:])
+            nc.gpsimd.tensor_tensor(out=y[:], in0=faded_sb[:], in1=windows[j % WINDOWS][:, 0:BANK], op=ALU.add)
+            nc.sync.dma_start(out=out[P * j : P * (j + 1), 0:BANK], in_=y[:])
+
+        def finish_right(j):
+            faded = turn_back(j, 1, ("T1", "T0", "T2", "T3")[j])
+            y = sb("y_right%d" % j, [P, BANK], F32)
+            nc.vector.tensor_tensor(out=y[:], in0=faded[:], in1=windows[j % WINDOWS][:, BANK:U], op=ALU.add)
+            nc.scalar.dma_start(out=out[P * j : P * (j + 1), BANK:U], in_=y[:])
+
+        last = len(pieces) - 1
+        for n in range(last):
+            scatter(n)
+        for c in range(6, 8):
             fade_block(c)
-        back_tags = (("T2", "T3"), ("T1", "T0"), ("A0", "A1"), ("C0", "C1"))
-
-        def scatter(j):
-            nc.vector.tensor_copy(out=placed[j][:].indirect(place_list[:]), in_=gk_sb[j][:])
-
-        def finish(j):
-            for h in range(2):
-                faded = bank(back_tags[j][h], "faded%d_%d" % (j, h))
-                for c in range(4):
-                    nc.tensor.transpose(faded[:, P * c : P * (c + 1)],
-                                        faded_t[2 * h + c // 2][:, c % 2, P * j : P * (j + 1)], ident[:])
-                y = sb("y%d_%d" % (j, h), [P, BANK], F32)
-                nc.vector.tensor_tensor(out=y[:], in0=faded[:], in1=placed[j][:, BANK * h : BANK * (h + 1)], op=ALU.add)
-                nc.sync.dma_start(out=out[P * j : P * (j + 1), BANK * h : BANK * (h + 1)], in_=y[:])
-
-        for j in range(PACK):
-            scatter(j)
-        for j in range(PACK):
-            finish(j)
+        for j in range(WINDOWS):
+            finish_left(j)
+        for j in range(WINDOWS - 1):
+            finish_right(j)
+        scatter(last)
+        finish_left(PACK - 1)
+        for j in range(WINDOWS - 1, PACK):
+            finish_right(j)

from contextlib import ExitStack

import concourse.mybir as mybir
from concourse.masks import make_identity

D, E, T, I, Q, U = 512, 512, 2048, 256, 512, 1024
FLOPS = 2 * (D * Q * I + E * Q * I + Q * D * I)
BYTES = 4 * (D * Q + E * Q + Q * D + 2 * D * U + T + U + 2 * Q) + 2 * (128 * 2 * T + 16 * T) + 2 * 128 * 16 * 2

F32 = mybir.dt.float32
BF16 = mybir.dt.bfloat16
I32 = mybir.dt.int32
U32 = mybir.dt.uint32
U16 = mybir.dt.uint16
U8 = mybir.dt.uint8
FP8X4 = mybir.dt.float8_e4m3fn_x4
FP4X4 = mybir.dt.float4_e2m1fn_x4
ALU = mybir.AluOpType
ACT = mybir.ActivationFunctionType
AX = mybir.AxisListType

P = 128
PACK = 4
BANK = 512
HALF = 256
LINE = 4
WINDOWS = 3


def tile_attend_bpriorpull_k_kernel(tc, query, keys_words, keys_scales, lprior, strict, gout, vals_words,
                                     vals_scales, qs, qrows, old, fade, offs, offs4, out):
    nc = tc.nc
    with ExitStack() as ctx:
        keep = ctx.enter_context(tc.tile_pool(name="keep", bufs=1))
        psum = ctx.enter_context(tc.psum_pool(name="psum", bufs=1))

        def sb(name, shape, dtype, reuse=None):
            return keep.tile(shape, dtype, name=name, tag=reuse or name, align_bytes=64)

        def bank(tag, name):
            return psum.tile([P, BANK], F32, name=name, tag=tag)

        slot_list = keep.tile([P, I // 16], U16, name="slot_list")
        place_list = keep.tile([P, I // 16], U16, name="place_list")

        key_bytes = sb("key_bytes", [P, T], U8)
        val_bytes = sb("val_bytes", [P, T], U8)
        prior_pool = sb("prior_pool", [P, T], F32)
        fade_rows = sb("fade_rows", [P, P], F32)
        windows = [sb("window%d" % w, [P, U], F32) for w in range(WINDOWS)]
        ident = sb("ident", [P, P], F32)

        nc.vector.memset(prior_pool[:].bitcast(I32), 0)
        nc.gpsimd.memset(fade_rows[:], 0.0)
        make_identity(nc, ident[:])
        for window in windows:
            nc.vector.memset(window[:].bitcast(I32), 0)

        def load_scale_rows(tile, scales):
            for g in range(4):
                rows = scales[0, 4 * g : 4 * g + 4, :].bitcast(I32)
                nc.sync.dma_start(out=tile[32 * g : 32 * (g + 1), :].bitcast(I32),
                                  in_=rows.unsqueeze(0).to_broadcast([8, 4, T // 4]))

        def load_half(name, src, h):
            half = sb("%s%d" % (name, h), [P, PACK, HALF], F32)
            nc.sync.dma_start(out=half[:], in_=src.rearrange("(p t) c -> p t c", t=PACK)[:, :, HALF * h : HALF * (h + 1)])
            return half

        key_words = sb("key_words", [P, T], U16)
        val_words = sb("val_words", [P, T], U16)
        strict_sb = sb("strict_sb", [P, PACK], F32)
        qs_sb = sb("qs_sb", [P, PACK], F32)
        nc.sync.dma_start(out=slot_list[:], in_=offs)
        prior_row = sb("prior_row", [1, T], F32)
        nc.sync.dma_start(out=prior_row[:], in_=lprior[0:1, :])
        query_raw = [load_half("query_raw", query, 0)]
        load_scale_rows(key_bytes, keys_scales)
        query_raw.append(load_half("query_raw", query, 1))
        nc.sync.dma_start(out=key_words[:].bitcast(I32), in_=keys_words[0].bitcast(I32))
        nc.sync.dma_start(out=val_words[:].bitcast(I32), in_=vals_words[0].bitcast(I32))
        gout_raw = [load_half("gout_raw", gout, 0)]
        load_scale_rows(val_bytes, vals_scales)
        gout_raw.append(load_half("gout_raw", gout, 1))
        qrows_raw = [load_half("qrows_raw", qrows, 0)]
        nc.sync.dma_start(out=strict_sb[:], in_=strict.rearrange("(p r) o -> p (r o)", r=PACK))
        qrows_raw.append(load_half("qrows_raw", qrows, 1))
        nc.sync.dma_start(out=qs_sb[:], in_=qs.rearrange("(p r) o -> p (r o)", r=PACK))
        nc.sync.dma_start(out=fade_rows[0 : U // P, :], in_=fade.rearrange("o (c p) -> (o c) p", p=P))
        old_view = old.rearrange("(j p) u -> p j u", p=P)
        old_sb = []
        for h in range(2):
            part = sb("old%d" % h, [P, PACK, BANK], F32)
            nc.sync.dma_start(out=part[:], in_=old_view[:, :, BANK * h : BANK * (h + 1)])
            old_sb.append(part)
        nc.sync.dma_start(out=place_list[:], in_=offs4)

        def gather(name, pool_tile, dtype):
            picked = sb(name, [P, I], dtype)
            nc.vector.tensor_copy(out=picked[:], in_=pool_tile[:].indirect(slot_list[:]))
            return picked

        def quantise(name, grouped):
            codes = sb(name + "_codes", [P, Q], U32)
            scales = sb(name + "_scales", [P, Q], U8)
            nc.vector.quantize_mx(out=codes[:].bitcast(FP8X4), scales=scales[:], in_=grouped[:])
            return codes, scales

        def deal(name, halves):
            grouped = sb(name, [P, PACK * Q], BF16)
            view = grouped[:].rearrange("p (r m e t) -> p m t e r", r=PACK, e=2, t=PACK)
            for h, copy in enumerate((nc.scalar.copy, nc.vector.tensor_copy)):
                copy(out=view[:, 32 * h : 32 * (h + 1)],
                     in_=halves[h][:].rearrange("p t (m e r) -> p m t e r", e=2, r=PACK))
            return grouped

        def scores(tags, name, codes, scales, words, word_scales):
            banks = [bank(tags[h], "%s%d" % (name, h)) for h in range(2)]
            tiles = []
            for r in range(PACK):
                dst = banks[r // 2][:, I * (r % 2) : I * (r % 2 + 1)]
                nc.tensor.matmul_mx(out=dst, lhsT=codes[:, P * r : P * (r + 1)].bitcast(FP8X4),
                                    lhsT_scale=scales[:, P * r : P * (r + 1)], rhs=words[:].bitcast(FP4X4),
                                    rhs_scale=word_scales[:], start=True, stop=True)
                tiles.append(dst)
            return banks, tiles

        nc.scalar.activation(out=prior_pool[0:1, :], in_=prior_row[:], func=ACT.Copy)
        key_s = gather("key_s", key_bytes, U8)
        prior_g = gather("prior_g", prior_pool, F32)
        q_codes, q_scales = quantise("q", deal("q_bf", query_raw))
        key_w = gather("key_w", key_words, U16)
        a_banks, a = scores(("A0", "A1"), "a", q_codes, q_scales, key_w, key_s)
        val_w = gather("val_w", val_words, U16)

        turn = bank("T0", "turn")
        for h in range(2):
            nc.tensor.transpose(turn[:, P * h : P * (h + 1)], prior_g[:, P * h : P * (h + 1)], ident[:])
        prior_col = sb("prior_col", [P, 2], F32)
        nc.scalar.copy(out=prior_col[:], in_=turn[:, 0 : 2 * P : P])
        spread = bank("T1", "spread")
        for h in range(2):
            nc.tensor.transpose(spread[:, P * h : P * (h + 1)], prior_col[:, h : h + 1].to_broadcast([P, P]), ident[:])
        prior_all = sb("prior_all", [P, I], F32)
        nc.scalar.copy(out=prior_all[:], in_=spread[:, 0:I])

        neg_max = sb("neg_max", [P, PACK], F32)
        z = sb("z", [P, PACK], F32)
        for h in range(2):
            nc.vector.tensor_reduce(out=neg_max[:, 2 * h : 2 * h + 2],
                                    in_=a_banks[h][:].rearrange("p (r i) -> p r i", r=2),
                                    axis=AX.X, op=ALU.max, negate=True)
        val_s = gather("val_s", val_bytes, U8)
        g_bf = deal("g_bf", gout_raw)
        p = sb("p", [P, PACK, I], F32, reuse="gout_raw0")
        for r in range(PACK):
            nc.scalar.activation(out=p[:, r, :], in_=a[r], func=ACT.Exp, bias=neg_max[:, r : r + 1],
                                 accum_out=z[:, r : r + 1])
        g_codes, g_scales = quantise("g", g_bf)
        c0 = scores(("C0", "C1"), "c", g_codes, g_scales, val_w, val_s)[1]

        gap = sb("gap", [P, PACK, I], F32, reuse="g_bf")
        for h in range(2):
            nc.vector.tensor_tensor(out=gap[:, 2 * h : 2 * h + 2, :], in0=a_banks[h][:].rearrange("p (r i) -> p r i", r=2),
                                    in1=prior_all[:].unsqueeze(1).to_broadcast([P, 2, I]), op=ALU.subtract)
        inv_z = sb("inv_z", [P, PACK], F32)
        nc.vector.reciprocal(out=inv_z[:], in_=z[:])
        neg_scale = sb("neg_scale", [P, PACK], F32)
        neg_h = sb("neg_h", [P, PACK, I], F32)

        def pull(r):
            nc.vector.scalar_tensor_tensor(out=neg_h[:, r, :], in0=gap[:, r, :], scalar=strict_sb[:, r : r + 1],
                                           in1=c0[r], op0=ALU.mult, op1=ALU.subtract)

        pull(0)
        nc.vector.scalar_tensor_tensor(out=neg_scale[:], in0=inv_z[:], scalar=-1.0, in1=qs_sb[:],
                                       op0=ALU.mult, op1=ALU.mult)
        for r in range(1, PACK):
            pull(r)

        rows_bf = sb("rows_bf", [P, PACK * D], BF16)
        rows_view = rows_bf[:].rearrange("p (c i t) -> p c t i", i=LINE, t=PACK)
        for h in range(2):
            nc.scalar.copy(out=rows_view[:, 64 * h : 64 * (h + 1)],
                           in_=qrows_raw[h][:].rearrange("p t (c i) -> p c t i", i=LINE))

        fade_turn = bank("T0", "fade_turn")
        nc.tensor.transpose(fade_turn[:, 0:P], fade_rows[:], ident[:])
        fade_col = sb("fade_col", [P, U // P], F32)
        nc.scalar.copy(out=fade_col[:], in_=fade_turn[:, 0 : U // P])
        faded_t = []
        stage_tags = ("T2", "T3", "T1", "T0", "T2", "T3", "C0", "C1")
        faded_reuse = (None, "neg_h", "gout_raw0", None)

        def fade_block(c):
            if c % 2 == 0:
                faded_t.append(sb("faded_t%d" % (c // 2), [P, 2, D], F32, reuse=faded_reuse[c // 2]))
            stage = bank(stage_tags[c], "stage%d" % c)
            for j in range(PACK):
                nc.tensor.transpose(stage[:, P * j : P * (j + 1)],
                                    old_sb[c // 4][:, j, P * (c % 4) : P * (c % 4 + 1)], ident[:])
            nc.scalar.activation(out=faded_t[c // 2][:, c % 2, :], in_=stage[:], func=ACT.Copy,
                                 scale=fade_col[:, c : c + 1])

        for c in range(2):
            fade_block(c)

        pm = sb("pm", [P, PACK, I], F32, reuse="qrows_raw1")
        ph = sb("ph", [P, PACK, I], F32)
        total = sb("total", [P, PACK], F32)
        mean = sb("mean", [P, PACK], F32)

        def weigh(r):
            nc.vector.scalar_tensor_tensor(out=ph[:, r, :], in0=neg_h[:, r, :], scalar=neg_scale[:, r : r + 1],
                                           in1=p[:, r, :], op0=ALU.mult, op1=ALU.mult,
                                           accum_out=total[:, r : r + 1])

        for lo, hi in ((0, 2), (2, 3)):
            for r in range(lo, hi):
                weigh(r)
            nc.vector.tensor_tensor(out=mean[:, lo:hi], in0=total[:, lo:hi], in1=inv_z[:, lo:hi], op=ALU.mult)
            for r in range(lo, hi):
                nc.scalar.activation(out=pm[:, r, :], in_=p[:, r, :], func=ACT.Copy, scale=mean[:, r : r + 1])
        weigh(3)
        r_codes = sb("r_codes", [P, D], U32)
        r_scales = sb("r_scales", [P, D], U8)

        def quantise_rows(h):
            cols = slice(HALF * h, HALF * (h + 1))
            nc.vector.quantize_mx(out=r_codes[:, cols].bitcast(FP8X4), scales=r_scales[:, cols],
                                  in_=rows_bf[:, PACK * cols.start : PACK * cols.stop])

        quantise_rows(0)
        nc.vector.tensor_scalar(out=pm[:, 3, :], in0=p[:, 3, :], scalar1=total[:, 3:4], scalar2=inv_z[:, 3:4],
                                op0=ALU.mult, op1=ALU.mult)

        gs_bf = sb("gs_bf", [P, PACK * I], BF16)
        gs_codes = sb("gs_codes", [P, I], U32)
        gs_scales = sb("gs_scales", [P, I], U8)
        for h in range(2):
            lines = slice(32 * h, 32 * (h + 1))
            nc.vector.tensor_tensor(out=gs_bf[:].rearrange("p (c i r) -> p c r i", i=LINE, r=PACK)[:, lines],
                                    in0=ph[:].rearrange("p r (c i) -> p c r i", i=LINE)[:, lines],
                                    in1=pm[:].rearrange("p r (c i) -> p c r i", i=LINE)[:, lines],
                                    op=ALU.subtract)
        for h in range(2):
            nc.vector.quantize_mx(out=gs_codes[:, P * h : P * (h + 1)].bitcast(FP8X4),
                                  scales=gs_scales[:, P * h : P * (h + 1)],
                                  in_=gs_bf[:, PACK * P * h : PACK * P * (h + 1)])
        quantise_rows(1)

        for c in range(2, 6):
            fade_block(c)

        pieces = ((0, 0, P), (1, 0, P), (0, P, I), (1, P, I), (2, 0, I), (3, 0, I))
        piece_tags = ("A0", "A1", "C0", "C1", "A0", "A1")
        gk_sb = []
        for n, (j, lo, hi) in enumerate(pieces):
            acc = bank(piece_tags[n], "gk%d" % n)
            nc.tensor.matmul_mx(out=acc[:, 0 : hi - lo], lhsT=r_codes[:, P * j : P * (j + 1)].bitcast(FP8X4),
                                lhsT_scale=r_scales[:, P * j : P * (j + 1)], rhs=gs_codes[:, lo:hi].bitcast(FP8X4),
                                rhs_scale=gs_scales[:, lo:hi], start=True, stop=True)
            gk = sb("gk_sb%d" % n, [P, hi - lo], F32)
            nc.scalar.copy(out=gk[:], in_=acc[:, 0 : hi - lo])
            gk_sb.append(gk)

        def scatter(n):
            j, lo, hi = pieces[n]
            nc.vector.tensor_copy(out=windows[j % WINDOWS][:].indirect(place_list[:, lo // 16 : hi // 16]),
                                  in_=gk_sb[n][:])

        def turn_back(j, h, tag):
            faded = bank(tag, "faded%d_%d" % (j, h))
            for c in range(4):
                nc.tensor.transpose(faded[:, P * c : P * (c + 1)],
                                    faded_t[2 * h + c // 2][:, c % 2, P * j : P * (j + 1)], ident[:])
            return faded

        def finish_left(j):
            faded = turn_back(j, 0, ("A0", "A1", "C0", "C1")[j])
            y = sb("y_left%d" % j, [P, BANK], F32)
            faded_sb = sb("faded_sb%d" % j, [P, BANK], F32)
            nc.scalar.copy(out=faded_sb[:], in_=faded[:])
            nc.gpsimd.tensor_tensor(out=y[:], in0=faded_sb[:], in1=windows[j % WINDOWS][:, 0:BANK], op=ALU.add)
            nc.sync.dma_start(out=out[P * j : P * (j + 1), 0:BANK], in_=y[:])

        def finish_right(j):
            faded = turn_back(j, 1, ("T1", "T0", "T2", "T3")[j])
            y = sb("y_right%d" % j, [P, BANK], F32)
            nc.vector.tensor_tensor(out=y[:], in0=faded[:], in1=windows[j % WINDOWS][:, BANK:U], op=ALU.add)
            nc.scalar.dma_start(out=out[P * j : P * (j + 1), BANK:U], in_=y[:])

        last = len(pieces) - 1
        for n in range(last):
            scatter(n)
        for c in range(6, 8):
            fade_block(c)
        for j in range(WINDOWS):
            finish_left(j)
        for j in range(WINDOWS - 1):
            finish_right(j)
        scatter(last)
        finish_left(PACK - 1)
        for j in range(WINDOWS - 1, PACK):
            finish_right(j)
